import numpy as np
import ml_dtypes


def mxq(x, axis, fmt="e4m3"):
    dtype, down = {"e4m3": (ml_dtypes.float8_e4m3fn, 7), "e5m2": (ml_dtypes.float8_e5m2, 14)}[fmt]
    v = np.moveaxis(np.asarray(x, np.float32).astype(ml_dtypes.bfloat16).astype(np.float64), axis, -1)
    blocks = v.reshape(v.shape[:-1] + (-1, 32))
    amax = np.abs(blocks).max(-1, keepdims=True)
    byte = np.maximum(np.where(amax > 0, np.frexp(amax)[1] - 1 + 127, 0) - down, 1)
    scale = np.exp2(byte - 127.0)
    codes = (blocks / scale).astype(np.float32).astype(dtype).astype(np.float64)
    return np.moveaxis((codes * scale).reshape(v.shape), -1, axis)


WIDE = False


def mx_kscale(k):
    if not WIDE:
        return np.ones(k)
    levels = np.array([10, -10, 5, -5, 0])
    if k % 512:
        return np.exp2(np.random.permutation(np.resize(levels, k // 32))).repeat(32)
    a = np.empty((k // 512, 16))
    for p in range(k // 512):
        a[p, :8] = np.random.permutation(np.resize(levels, 8))
        for g in range(8):
            far = levels[np.abs(levels - a[p, g]) >= 10]
            a[p, g + 8] = far[np.random.randint(len(far))]
    return np.exp2(a.ravel()).repeat(32)


def f64(x):
    return np.asarray(x).astype(np.float64)


def striped(idx):
    return np.tile(np.asarray(idx).reshape(-1, 16).T, (8, 1)).astype(np.uint16)


def unstriped(offs):
    return offs[:16].T.reshape(-1).astype(np.int64)


E2M1 = np.array([0.0, 0.5, 1.0, 1.5, 2.0, 3.0, 4.0, 6.0, -0.0, -0.5, -1.0, -1.5, -2.0, -3.0, -4.0, -6.0])


def pack_weight(w, fmt):
    k, n = w.shape
    w = f64(np.asarray(w, np.float32).astype(ml_dtypes.bfloat16)).reshape(k // 32, 32, n)
    amax = np.abs(w).max(1)
    if fmt == "e4m3":
        byte = np.frexp(amax)[1] - 1 + 127 - 7
    else:
        mant, ex = np.frexp(amax / 6.0)
        byte = np.where(mant > 0.5, ex, ex - 1) + 127
    byte = np.clip(np.where(amax > 0, byte, 1), 1, 254)
    scaled = (w * np.exp2(127.0 - byte)[:, None, :]).reshape(k, n).astype(np.float32)
    by_word = np.ascontiguousarray(scaled.reshape(k // 512, 128, 4, n).transpose(0, 1, 3, 2))
    if fmt == "e4m3":
        words = by_word.astype(ml_dtypes.float8_e4m3fn).view(np.uint8)
    else:
        c = by_word.astype(ml_dtypes.float4_e2m1fn).view(np.uint8) & 0xF
        words = (c[..., 0::2] | (c[..., 1::2] << 4)).reshape(k // 512, 128, 2 * n)
    return np.ascontiguousarray(words), np.ascontiguousarray(byte.astype(np.uint8).reshape(k // 512, 16, n))


def unpack_weight(words, scales, fmt):
    g, _, n = scales.shape
    words = np.ascontiguousarray(words).reshape(g, 128, n, -1)
    if fmt == "e4m3":
        vals = words.view(ml_dtypes.float8_e4m3fn).astype(np.float64)
    else:
        nib = np.empty((g, 128, n, 4), np.uint8)
        nib[..., 0::2] = words & 0xF
        nib[..., 1::2] = words >> 4
        vals = E2M1[nib]
    vals = vals * np.repeat(np.exp2(scales.astype(np.float64) - 127.0), 8, axis=1)[..., None]
    return vals.transpose(0, 1, 3, 2).reshape(g * 512, n)


def sigmoid(v):
    return 1.0 / (1.0 + np.exp(-v))


D, E, T, I, Q, U = 512, 512, 2048, 512, 128, 1024


def setup_inputs():
    n = np.random.standard_normal
    idx2 = np.random.permutation(U)[:I]
    idx4 = np.random.permutation(I)[:I]
    idx = np.random.permutation(T)[:I]
    fd = mx_kscale(D)
    fe = mx_kscale(E)
    keysp = pack_weight(n((D, T)) / fd[:, None], "e4m3")
    valsp = pack_weight(n((E, T)) / fe[:, None], "e4m3")
    return {
        "query": (n((D, Q)) * 1.2 / np.sqrt(D) * fd[:, None]).astype(np.float32),
        "query2": (n((D, Q)) * 1.5 / np.sqrt(D) * fd[:, None]).astype(np.float32),
        "keys_words": keysp[0],
        "keys_scales": keysp[1],
        "notes": (n((D, U)) / fd[:, None]).astype(np.float32),
        "lam": (np.random.uniform(-0.8, 0.8, (Q, 1))).astype(np.float32),
        "rival": (np.random.uniform(0.5, 2.0, (Q, 1))).astype(np.float32),
        "gout": (n((E, Q)) * 1 / np.sqrt(E) * fe[:, None]).astype(np.float32),
        "vals_words": valsp[0],
        "vals_scales": valsp[1],
        "dquery": (n((D, Q)) * 1.0 / np.sqrt(D) * fd[:, None]).astype(np.float32),
        "base": (0.5 * n((Q, T))).astype(np.float32),
        "offs2": striped(idx2),
        "offs4": striped(idx4),
        "offs": striped(idx),
    }


def reference(query, query2, keys_words, keys_scales, notes, lam, rival, gout, vals_words, vals_scales, dquery, base, offs2, offs4, offs):
    idx2 = unstriped(offs2)
    idx4 = unstriped(offs4)
    idx = unstriped(offs)
    keysu = unpack_weight(keys_words, keys_scales, "e4m3")
    valsu = unpack_weight(vals_words, vals_scales, "e4m3")
    queryq = mxq(f64(query), 0, "e4m3")
    keysidxg = keysu[:, idx]
    a = queryq.T @ keysidxg
    dqueryq = mxq(f64(dquery), 0, "e4m3")
    ta = dqueryq.T @ keysidxg
    query2q = mxq(f64(query2), 0, "e4m3")
    notesidx2q = mxq(f64(notes)[:, idx2], 0, "e4m3")
    b = query2q.T @ notesidx2q
    g1 = sigmoid(b)
    s = a * g1 + (1.0 - g1) * f64(lam)
    p = np.exp(s)
    r = p / (p + p[:, idx4] * f64(rival))
    goutq = mxq(f64(gout), 0, "e4m3")
    valsidxg = valsu[:, idx]
    c0 = goutq.T @ valsidxg
    dr = c0 / np.sum(r, axis=1, keepdims=True) + np.sum(c0 * r / np.square(np.sum(r, axis=1, keepdims=True)) * (-1.0), axis=1, keepdims=True)
    e1 = dr * p / np.square(p + p[:, idx4] * f64(rival)) * (-1.0) * f64(rival)
    s1 = np.zeros((Q, I))
    s1[:, idx4] = e1
    dp = dr / (p + p[:, idx4] * f64(rival)) + s1 - dr * p / np.square(p + p[:, idx4] * f64(rival))
    ts = ta * g1
    tp = ts * p
    tr = (tp - (tp + tp[:, idx4] * f64(rival)) * p / (p + p[:, idx4] * f64(rival))) / (p + p[:, idx4] * f64(rival))
    tdr = np.sum(tr, axis=1, keepdims=True) * c0 / np.square(np.sum(r, axis=1, keepdims=True)) * (-1.0) + np.sum((tr * c0 - np.sum(tr, axis=1, keepdims=True) * np.sum(r, axis=1, keepdims=True) * 2.0 * c0 * r / np.square(np.sum(r, axis=1, keepdims=True))) / np.square(np.sum(r, axis=1, keepdims=True)) * (-1.0), axis=1, keepdims=True)
    te1 = (tdr * p + tp * dr - (tp + tp[:, idx4] * f64(rival)) * (p + p[:, idx4] * f64(rival)) * 2.0 * dr * p / np.square(p + p[:, idx4] * f64(rival))) / np.square(p + p[:, idx4] * f64(rival)) * (-1.0) * f64(rival)
    ts1 = np.zeros((Q, I))
    ts1[:, idx4] = te1
    tdp = (tdr - (tp + tp[:, idx4] * f64(rival)) * dr / (p + p[:, idx4] * f64(rival))) / (p + p[:, idx4] * f64(rival)) + ts1 - (tdr * p + tp * dr - (tp + tp[:, idx4] * f64(rival)) * (p + p[:, idx4] * f64(rival)) * 2.0 * dr * p / np.square(p + p[:, idx4] * f64(rival))) / np.square(p + p[:, idx4] * f64(rival))
    tds = tdp * p + tp * dp
    tda = tds * g1
    gs = tda * 512.0
    gf = np.zeros((Q, T))
    gf[:, idx] = gs
    y = f64(base) + gf
    return y

@@ -1,0 +1,273 @@
+from contextlib import ExitStack
+
+import concourse.mybir as mybir
+
+D, T, I, Q, U = 512, 2048, 512, 128, 1024
+FLOPS = 4 * 2 * D * Q * I
+
+F32 = mybir.dt.float32
+BF16 = mybir.dt.bfloat16
+I32 = mybir.dt.int32
+U32 = mybir.dt.uint32
+U16 = mybir.dt.uint16
+U8 = mybir.dt.uint8
+FP8X4 = mybir.dt.float8_e4m3fn_x4
+ALU = mybir.AluOpType
+ACT = mybir.ActivationFunctionType
+
+P = 128
+PACK = 4
+SPARE = 16
+SCALAR_SLOTS = 320
+HALF = I // 2
+HALVES = (slice(0, HALF), slice(HALF, I))
+OUT_CUTS = (0, 256, 768, 1280, 1792, 2048)
+
+
+def tile_attend_hvtilted_overlinked_s_kernel(tc, query, query2, keys_words, keys_scales, notes, lam, rival, gout,
+                                              vals_words, vals_scales, dquery, base, offs2, offs4, offs, out):
+    nc = tc.nc
+    with ExitStack() as ctx:
+        sb = ctx.enter_context(tc.tile_pool(name="sb", bufs=1))
+        ps = ctx.enter_context(tc.psum_pool(name="ps", bufs=1))
+
+        def wide(name, cols=I):
+            return sb.tile([P, cols], F32, name=name, align_bytes=64)
+
+        def col(name):
+            return sb.tile([P, 1], F32, name=name)
+
+        def load_list(name, src):
+            t = sb.tile([P, I // 16], U16, name=name)
+            nc.sync.dma_start(t[:], src)
+            return t
+
+        def load_rows(name, src):
+            t = sb.tile([P, PACK, Q], F32, name=name, align_bytes=64)
+            nc.sync.dma_start(t[:], src.rearrange("(p j) w -> p j w", j=PACK))
+            return t
+
+        def load_words(name, src):
+            t = sb.tile([P, T], I32, name=name, align_bytes=64)
+            nc.sync.dma_start(t[:], src[0].rearrange("p n t -> p (n t)").bitcast(I32))
+            return t
+
+        def load_scales(name, src):
+            t = sb.tile([P, T], U8, name=name, align_bytes=64)
+            nc.gpsimd.memset(t[:].bitcast(I32), 0)
+            for quad in range(4):
+                nc.sync.dma_start(t[32 * quad:32 * quad + 4, :].bitcast(I32),
+                                    src[0, 4 * quad:4 * quad + 4, :].bitcast(I32))
+            return t
+
+        def weave_views(dst, src):
+            return (dst.rearrange("p (c i) t -> p c t i", i=4), src.rearrange("p t (c i) -> p c t i", i=4))
+
+        def quantize(name, woven, cols):
+            codes = sb.tile([P, cols], U32, name=name + "_codes", align_bytes=64)
+            scales = sb.tile([P, cols], U8, name=name + "_scales", align_bytes=64)
+            nc.vector.quantize_mx(out=codes[:].bitcast(FP8X4), scales=scales[:],
+                                  in_=woven[:].rearrange("p w j -> p (w j)"))
+            return codes[:], scales[:]
+
+        def weave_rows(name, raw, on_scalar):
+            woven = sb.tile([P, Q, PACK], BF16, name=name + "_woven", align_bytes=64)
+            dst, src = weave_views(woven[:], raw[:])
+            if on_scalar:
+                nc.scalar.activation(dst, src, ACT.Copy)
+            else:
+                nc.vector.tensor_copy(dst, src)
+            return woven
+
+        def product(name, rows, cols, width):
+            acc = ps.tile([P, width], F32, name=name)
+            nc.tensor.matmul_mx(out=acc[:], lhsT=rows[0].bitcast(FP8X4), lhsT_scale=rows[1],
+                                rhs=cols[0].bitcast(FP8X4), rhs_scale=cols[1], start=True, stop=True)
+            return acc
+
+        def entries(lst, slots):
+            return lst[:, slots.start // 16:slots.stop // 16]
+
+        def load_plane(t):
+            plane = wide("plane%d" % t, U)
+            nc.sync.dma_start(plane[:], notes.rearrange("(p j) u -> p j u", j=PACK)[:, t, :])
+            return plane
+
+        list2 = load_list("list2", offs2)
+        planes = [load_plane(0)]
+        list0 = load_list("list0", offs)
+        list4 = load_list("list4", offs4)
+        lam_c = col("lam_c")
+        nc.sync.dma_start(lam_c[:], lam)
+        rival_c = col("rival_c")
+        nc.sync.dma_start(rival_c[:], rival)
+        planes.append(load_plane(1))
+        planes.append(load_plane(2))
+        keys_sc = load_scales("keys_sc", keys_scales)
+        planes.append(load_plane(3))
+        vals_sc = load_scales("vals_sc", vals_scales)
+        query2_raw = load_rows("query2_raw", query2)
+        query_raw = load_rows("query_raw", query)
+        keys_w = load_words("keys_w", keys_words)
+        dquery_raw = load_rows("dquery_raw", dquery)
+        gout_raw = load_rows("gout_raw", gout)
+        vals_w = load_words("vals_w", vals_words)
+        base_sb = wide("base_sb", T)
+        nc.sync.dma_start(base_sb[:], base)
+
+        p = wide("p", I + SPARE)
+        tp = wide("tp", I + SPARE)
+        back_s = wide("back_s")
+        back_v = wide("back_v")
+        gf = wide("gf", T)
+        nc.vector.memset(p[:, I:], 0.0)
+        nc.vector.memset(tp[:, I:], 0.0)
+        nc.vector.memset(back_s[:], 0.0)
+        nc.vector.memset(back_v[:], 0.0)
+        nc.vector.memset(gf[:], 0.0)
+
+        keys_sc_g = sb.tile([P, I], U8, name="keys_sc_g", align_bytes=64)
+        nc.vector.tensor_copy(keys_sc_g[:], keys_sc[:].indirect(list0[:]))
+
+        vals_sc_g = sb.tile([P, I], U8, name="vals_sc_g", align_bytes=64)
+        nc.vector.tensor_copy(vals_sc_g[:], vals_sc[:].indirect(list0[:]))
+        notes_g = sb.tile([P, PACK, I], BF16, name="notes_g", align_bytes=64)
+        for t in range(PACK - 1):
+            nc.scalar.activation(notes_g[:, t, :], planes[t][:].indirect(list2[:]), ACT.Copy)
+        for h in HALVES:
+            nc.scalar.activation(notes_g[:, PACK - 1, h], planes[PACK - 1][:].indirect(entries(list2, h)), ACT.Copy)
+        query2_woven = weave_rows("query2", query2_raw, True)
+        query_woven = weave_rows("query", query_raw, True)
+        notes_woven = []
+        for k, h in enumerate(HALVES):
+            woven = sb.tile([P, HALF, PACK], BF16, name="notes_woven%d" % k, align_bytes=64)
+            nc.vector.tensor_copy(*weave_views(woven[:], notes_g[:, :, h]))
+            notes_woven.append(woven)
+        query2_q = quantize("query2", query2_woven, Q)
+        b = [product("b%d" % k, query2_q, quantize("notes%d" % k, notes_woven[k], HALF), HALF) for k in range(2)]
+        query_q = quantize("query", query_woven, Q)
+
+        tanh_b = wide("tanh_b")
+        gate = wide("gate")
+        for k, h in enumerate(HALVES):
+            nc.scalar.activation(tanh_b[:, h], b[k][:], ACT.Tanh, scale=0.5)
+        for h in HALVES:
+            nc.scalar.activation(gate[:, h], tanh_b[:, h], ACT.Identity, scale=-0.5 / HALF, bias=-0.5 / HALF)
+        gout_woven = weave_rows("gout", gout_raw, True)
+
+        keys_w_g = sb.tile([P, I], U32, name="keys_w_g", align_bytes=64)
+        a = []
+        for k, h in enumerate(HALVES):
+            nc.vector.tensor_copy(keys_w_g[:, h], keys_w[:].bitcast(U32).indirect(entries(list0, h)))
+            a.append(product("a%d" % k, query_q, (keys_w_g[:, h], keys_sc_g[:, h]), HALF))
+        dquery_woven = weave_rows("dquery", dquery_raw, False)
+
+        y = wide("y")
+        shift = col("shift")
+        nc.vector.scalar_tensor_tensor(y[:, HALVES[0]], a[0][:], lam_c[:], gate[:, HALVES[0]], ALU.subtract, ALU.mult,
+                                       accum_out=shift[:])
+        dquery_q = quantize("dquery", dquery_woven, Q)
+        ta = product("ta", dquery_q, (keys_w_g[:], keys_sc_g[:]), I)
+        nc.vector.scalar_tensor_tensor(y[:, HALVES[1]], a[1][:], lam_c[:], gate[:, HALVES[1]], ALU.subtract, ALU.mult)
+        for h in HALVES:
+            nc.scalar.activation(p[:, h], y[:, h], ACT.Exp, scale=-float(HALF), bias=shift[:])
+        gout_q = quantize("gout", gout_woven, Q)
+        inv_rival = col("inv_rival")
+        nc.vector.reciprocal(inv_rival[:], rival_c[:])
+        pr = wide("pr")
+        den = wide("den")
+        root = wide("root")
+        inv = wide("inv")
+        for h in HALVES:
+            nc.vector.tensor_scalar(pr[:, h], p[:, h], inv_rival[:], None, ALU.mult)
+        for h in HALVES:
+            nc.vector.tensor_tensor(den[:, h], p[:].indirect(entries(list4, h)), pr[:, h], ALU.add)
+        for h in HALVES:
+            nc.scalar.activation(root[:, h], den[:, h], ACT.Abs_reciprocal_sqrt)
+        for h in HALVES:
+            nc.scalar.activation(inv[:, h], root[:, h], ACT.Square)
+        ts = wide("ts")
+        for h in HALVES:
+            nc.vector.tensor_tensor(ts[:, h], ta[:, h], gate[:, h], ALU.mult)
+        for h in HALVES:
+            nc.vector.tensor_tensor(tp[:, h], ts[:, h], p[:, h], ALU.mult)
+        tp_g = wide("tp_g")
+        for h in HALVES:
+            nc.scalar.activation(tp_g[:, h], tp[:].indirect(entries(list4, h)), ACT.Copy)
+
+        vals_w_g = sb.tile([P, I], U32, name="vals_w_g", align_bytes=64)
+        nc.vector.tensor_copy(vals_w_g[:], vals_w[:].bitcast(U32).indirect(list0[:]))
+        c0 = product("c0", gout_q, (vals_w_g[:], vals_sc_g[:]), I)
+
+        r = wide("r")
+        r_sum = col("r_sum")
+        nc.vector.scalar_tensor_tensor(r[:], pr[:], 1.0, inv[:], ALU.mult, ALU.mult, accum_out=r_sum[:])
+        tden = wide("tden")
+        for h in HALVES:
+            nc.vector.scalar_tensor_tensor(tden[:, h], tp[:, h], inv_rival[:], tp_g[:, h], ALU.mult, ALU.add)
+        alpha = col("alpha")
+        nc.vector.reciprocal(alpha[:], r_sum[:])
+        rc = wide("rc")
+        rc_sum = col("rc_sum")
+        nc.vector.scalar_tensor_tensor(rc[:], c0[:], -1.0, r[:], ALU.mult, ALU.mult, accum_out=rc_sum[:])
+        sq = wide("sq")
+        nc.scalar.activation(sq[:], r[:], ACT.Square, bias=-0.5)
+        neg_mu = col("neg_mu")
+        nc.scalar.activation(neg_mu[:], rc_sum[:], ACT.Identity, scale=alpha[:])
+        c1 = wide("c1")
+        nc.scalar.activation(c1[:], c0[:], ACT.Identity, bias=neg_mu[:])
+        m_scale = col("m_scale")
+        nc.scalar.activation(m_scale[:], alpha[:], ACT.Identity, scale=-0.5)
+        m_bias = col("m_bias")
+        nc.scalar.activation(m_bias[:], alpha[:], ACT.Identity, scale=0.125)
+        out_scale = col("out_scale")
+        nc.scalar.activation(out_scale[:], alpha[:], ACT.Identity, scale=-2.0 * 512.0 * HALF * HALF)
+        half_m = wide("half_m")
+        nc.scalar.activation(half_m[:], sq[:], ACT.Identity, scale=m_scale[:], bias=m_bias[:])
+        e = wide("e")
+        dd = wide("dd")
+        tr = wide("tr")
+        trc = wide("trc")
+        tr_part = [col("tr_part0"), col("tr_part1")]
+        trc_part = [col("trc_part0"), col("trc_part1")]
+        for h in HALVES:
+            nc.vector.tensor_tensor(e[:, h], tden[:, h], inv[:, h], ALU.mult)
+        for h in HALVES:
+            nc.vector.tensor_tensor(dd[:, h], ts[:, h], e[:, h], ALU.subtract)
+        for k, h in enumerate(HALVES):
+            nc.vector.scalar_tensor_tensor(tr[:, h], r[:, h], 1.0, dd[:, h], ALU.mult, ALU.mult, accum_out=tr_part[k][:])
+        for k, h in enumerate(HALVES):
+            nc.vector.scalar_tensor_tensor(trc[:, h], tr[:, h], 1.0, c1[:, h], ALU.mult, ALU.mult,
+                                           accum_out=trc_part[k][:])
+        tr_sum = col("tr_sum")
+        nc.scalar.activation(tr_sum[:], tr_part[0][:], ACT.Identity, bias=tr_part[1][:])
+        first = slice(0, SCALAR_SLOTS)
+        rest = slice(SCALAR_SLOTS, I)
+        c2 = wide("c2")
+        for h in (first, rest):
+            nc.scalar.activation(c2[:, h], c1[:, h], ACT.Identity, scale=tr_sum[:], bias=trc_part[0][:])
+        w = wide("w")
+        z = wide("z")
+        th = wide("th")
+        for h in (first, rest):
+            nc.vector.scalar_tensor_tensor(w[:, h], r[:, h], -0.5, trc[:, h], ALU.add, ALU.mult)
+        for h in (first, rest):
+            nc.vector.scalar_tensor_tensor(z[:, h], c2[:, h], trc_part[1][:], half_m[:, h], ALU.add, ALU.mult)
+        nc.vector.tensor_tensor(th[:, first], z[:, first], w[:, first], ALU.add)
+        nc.scalar.activation(back_s[:].indirect(entries(list4, first)), th[:, first], ACT.Copy)
+        out_gate = wide("out_gate")
+        nc.scalar.activation(out_gate[:], gate[:], ACT.Identity, scale=out_scale[:])
+        nc.vector.tensor_tensor(back_v[:].indirect(entries(list4, rest)), z[:, rest], w[:, rest], ALU.add)
+        nc.vector.tensor_tensor(th[:, rest], z[:, rest], w[:, rest], ALU.add)
+        d1 = wide("d1")
+        for h in (first, rest):
+            nc.vector.tensor_tensor(d1[:, h], th[:, h], back_v[:, h], ALU.subtract)
+        d2 = wide("d2")
+        nc.vector.tensor_tensor(d2[:], d1[:], back_s[:], ALU.subtract)
+        nc.vector.tensor_tensor(gf[:].indirect(list0[:]), d2[:], out_gate[:], ALU.mult)
+
+        for c in range(len(OUT_CUTS) - 1):
+            cols = slice(OUT_CUTS[c], OUT_CUTS[c + 1])
+            res = wide("res%d" % c, cols.stop - cols.start)
+            nc.vector.tensor_tensor(res[:], gf[:, cols], base_sb[:, cols], ALU.add)
+            nc.sync.dma_start(out[:, cols], res[:])

@@ -31,34 +31,36 @@ def tile_attend_hvtilted_overlinked_s_kernel(tc, query, query2, keys_words, keys
         sb = ctx.enter_context(tc.tile_pool(name="sb", bufs=1))
         ps = ctx.enter_context(tc.psum_pool(name="ps", bufs=1))
 
-        def wide(name, cols=I):
-            return sb.tile([P, cols], F32, name=name, align_bytes=64)
+        def wide(name, cols=I, tag=None):
+            return sb.tile([P, cols], F32, name=name, tag=tag or name, align_bytes=64)
 
-        def col(name):
-            return sb.tile([P, 1], F32, name=name)
+        def col(name, tag=None):
+            return sb.tile([P, 1], F32, name=name, tag=tag or name, align_bytes=64)
 
         def load_list(name, src):
             t = sb.tile([P, I // 16], U16, name=name)
             nc.sync.dma_start(t[:], src)
             return t
 
-        def load_rows(name, src):
-            t = sb.tile([P, PACK, Q], F32, name=name, align_bytes=64)
+        def load_rows(name, src, tag=None):
+            t = sb.tile([P, PACK, Q], F32, name=name, tag=tag or name, align_bytes=64)
             nc.sync.dma_start(t[:], src.rearrange("(p j) w -> p j w", j=PACK))
             return t
 
-        def load_words(name, src):
-            t = sb.tile([P, T], I32, name=name, align_bytes=64)
+        def load_words(name, src, tag=None):
+            t = sb.tile([P, T], I32, name=name, tag=tag or name, align_bytes=64)
             nc.sync.dma_start(t[:], src[0].rearrange("p n t -> p (n t)").bitcast(I32))
             return t
 
-        def load_scales(name, src):
+        def zeroed_plane(name):
             t = sb.tile([P, T], U8, name=name, align_bytes=64)
-            nc.gpsimd.memset(t[:].bitcast(I32), 0)
-            for quad in range(4):
-                nc.sync.dma_start(t[32 * quad:32 * quad + 4, :].bitcast(I32),
-                                    src[0, 4 * quad:4 * quad + 4, :].bitcast(I32))
+            nc.vector.memset(t[:].bitcast(I32), 0)
             return t
+
+        def load_scales(t, src, queue):
+            for quad in range(4):
+                queue.dma_start(t[32 * quad:32 * quad + 4, :].bitcast(I32),
+                                    src[0, 4 * quad:4 * quad + 4, :].bitcast(I32))
 
         def weave_views(dst, src):
             return (dst.rearrange("p (c i) t -> p c t i", i=4), src.rearrange("p t (c i) -> p c t i", i=4))
@@ -70,8 +72,8 @@ def tile_attend_hvtilted_overlinked_s_kernel(tc, query, query2, keys_words, keys
                                   in_=woven[:].rearrange("p w j -> p (w j)"))
             return codes[:], scales[:]
 
-        def weave_rows(name, raw, on_scalar):
-            woven = sb.tile([P, Q, PACK], BF16, name=name + "_woven", align_bytes=64)
+        def weave_rows(name, raw, on_scalar, tag=None):
+            woven = sb.tile([P, Q, PACK], BF16, name=name + "_woven", tag=tag or name + "_woven", align_bytes=64)
             dst, src = weave_views(woven[:], raw[:])
             if on_scalar:
                 nc.scalar.activation(dst, src, ACT.Copy)
@@ -93,27 +95,29 @@ def tile_attend_hvtilted_overlinked_s_kernel(tc, query, query2, keys_words, keys
             nc.sync.dma_start(plane[:], notes.rearrange("(p j) u -> p j u", j=PACK)[:, t, :])
             return plane
 
+        warm_in = col("warm_in")
+        nc.gpsimd.memset(warm_in[:], 0.0)
+        warm_out = col("warm_out")
+        nc.scalar.activation(warm_out[:], warm_in[:], ACT.Exp)
+        keys_sc = zeroed_plane("keys_sc")
+        vals_sc = zeroed_plane("vals_sc")
+        load_scales(vals_sc, vals_scales, nc.gpsimd)
         list2 = load_list("list2", offs2)
-        planes = [load_plane(0)]
+        planes = [load_plane(0), load_plane(1)]
+        load_scales(keys_sc, keys_scales, nc.sync)
         list0 = load_list("list0", offs)
-        list4 = load_list("list4", offs4)
-        lam_c = col("lam_c")
-        nc.sync.dma_start(lam_c[:], lam)
-        rival_c = col("rival_c")
-        nc.sync.dma_start(rival_c[:], rival)
-        planes.append(load_plane(1))
-        planes.append(load_plane(2))
-        keys_sc = load_scales("keys_sc", keys_scales)
-        planes.append(load_plane(3))
-        vals_sc = load_scales("vals_sc", vals_scales)
+        planes.extend([load_plane(2), load_plane(3)])
         query2_raw = load_rows("query2_raw", query2)
         query_raw = load_rows("query_raw", query)
         keys_w = load_words("keys_w", keys_words)
         dquery_raw = load_rows("dquery_raw", dquery)
+        lam_c = col("lam_c")
+        nc.sync.dma_start(lam_c[:], lam)
+        list4 = load_list("list4", offs4)
+        rival_c = col("rival_c")
+        nc.sync.dma_start(rival_c[:], rival)
         gout_raw = load_rows("gout_raw", gout)
         vals_w = load_words("vals_w", vals_words)
-        base_sb = wide("base_sb", T)
-        nc.sync.dma_start(base_sb[:], base)
 
         p = wide("p", I + SPARE)
         tp = wide("tp", I + SPARE)
@@ -129,8 +133,6 @@ def tile_attend_hvtilted_overlinked_s_kernel(tc, query, query2, keys_words, keys
         keys_sc_g = sb.tile([P, I], U8, name="keys_sc_g", align_bytes=64)
         nc.vector.tensor_copy(keys_sc_g[:], keys_sc[:].indirect(list0[:]))
 
-        vals_sc_g = sb.tile([P, I], U8, name="vals_sc_g", align_bytes=64)
-        nc.vector.tensor_copy(vals_sc_g[:], vals_sc[:].indirect(list0[:]))
         notes_g = sb.tile([P, PACK, I], BF16, name="notes_g", align_bytes=64)
         for t in range(PACK - 1):
             nc.scalar.activation(notes_g[:, t, :], planes[t][:].indirect(list2[:]), ACT.Copy)
@@ -153,63 +155,68 @@ def tile_attend_hvtilted_overlinked_s_kernel(tc, query, query2, keys_words, keys
             nc.scalar.activation(tanh_b[:, h], b[k][:], ACT.Tanh, scale=0.5)
         for h in HALVES:
             nc.scalar.activation(gate[:, h], tanh_b[:, h], ACT.Identity, scale=-0.5 / HALF, bias=-0.5 / HALF)
-        gout_woven = weave_rows("gout", gout_raw, True)
 
-        keys_w_g = sb.tile([P, I], U32, name="keys_w_g", align_bytes=64)
+        keys_q = []
         a = []
         for k, h in enumerate(HALVES):
-            nc.vector.tensor_copy(keys_w_g[:, h], keys_w[:].bitcast(U32).indirect(entries(list0, h)))
-            a.append(product("a%d" % k, query_q, (keys_w_g[:, h], keys_sc_g[:, h]), HALF))
-        dquery_woven = weave_rows("dquery", dquery_raw, False)
+            words = sb.tile([P, HALF], U32, name="keys_w_g%d" % k, tag="notes_woven%d" % k, align_bytes=64)
+            nc.vector.tensor_copy(words[:], keys_w[:].bitcast(U32).indirect(entries(list0, h)))
+            keys_q.append((words[:], keys_sc_g[:, h]))
+            a.append(product("a%d" % k, query_q, keys_q[k], HALF))
+        dquery_woven = weave_rows("dquery", dquery_raw, True, "tanh_b")
+
+        base_sb = wide("base_sb", T, "keys_w")
+        nc.sync.dma_start(base_sb[:], base)
 
         y = wide("y")
         shift = col("shift")
         nc.vector.scalar_tensor_tensor(y[:, HALVES[0]], a[0][:], lam_c[:], gate[:, HALVES[0]], ALU.subtract, ALU.mult,
                                        accum_out=shift[:])
-        dquery_q = quantize("dquery", dquery_woven, Q)
-        ta = product("ta", dquery_q, (keys_w_g[:], keys_sc_g[:]), I)
         nc.vector.scalar_tensor_tensor(y[:, HALVES[1]], a[1][:], lam_c[:], gate[:, HALVES[1]], ALU.subtract, ALU.mult)
         for h in HALVES:
             nc.scalar.activation(p[:, h], y[:, h], ACT.Exp, scale=-float(HALF), bias=shift[:])
-        gout_q = quantize("gout", gout_woven, Q)
-        inv_rival = col("inv_rival")
-        nc.vector.reciprocal(inv_rival[:], rival_c[:])
-        pr = wide("pr")
+        p_g = wide("p_g")
+        for h in HALVES:
+            nc.scalar.activation(p_g[:, h], p[:].indirect(entries(list4, h)), ACT.Copy)
+        warm_root = col("warm_root")
+        nc.scalar.activation(warm_root[:], p_g[:, I - 1:I], ACT.Abs_reciprocal_sqrt)
+        dquery_q = quantize("dquery", dquery_woven, Q)
+        ta = [product("ta%d" % k, dquery_q, keys_q[k], HALF) for k in range(2)]
+        vals_sc_g = sb.tile([P, I], U8, name="vals_sc_g", tag="lam_c", align_bytes=64)
+        nc.vector.tensor_copy(vals_sc_g[:], vals_sc[:].indirect(list0[:]))
         den = wide("den")
         root = wide("root")
         inv = wide("inv")
-        for h in HALVES:
-            nc.vector.tensor_scalar(pr[:, h], p[:, h], inv_rival[:], None, ALU.mult)
-        for h in HALVES:
-            nc.vector.tensor_tensor(den[:, h], p[:].indirect(entries(list4, h)), pr[:, h], ALU.add)
+        ts = wide("ts")
+        for k, h in enumerate(HALVES):
+            nc.vector.tensor_tensor(ts[:, h], ta[k][:], gate[:, h], ALU.mult)
+        nc.vector.scalar_tensor_tensor(den[:], p_g[:], rival_c[:], p[:, :I], ALU.mult, ALU.add)
         for h in HALVES:
             nc.scalar.activation(root[:, h], den[:, h], ACT.Abs_reciprocal_sqrt)
         for h in HALVES:
             nc.scalar.activation(inv[:, h], root[:, h], ACT.Square)
-        ts = wide("ts")
-        for h in HALVES:
-            nc.vector.tensor_tensor(ts[:, h], ta[:, h], gate[:, h], ALU.mult)
-        for h in HALVES:
-            nc.vector.tensor_tensor(tp[:, h], ts[:, h], p[:, h], ALU.mult)
-        tp_g = wide("tp_g")
+        nc.vector.tensor_tensor(tp[:, :I], ts[:], p[:, :I], ALU.mult)
+        tp_g = wide("tp_g", tag="root")
         for h in HALVES:
             nc.scalar.activation(tp_g[:, h], tp[:].indirect(entries(list4, h)), ACT.Copy)
 
-        vals_w_g = sb.tile([P, I], U32, name="vals_w_g", align_bytes=64)
+        gout_woven = weave_rows("gout", gout_raw, False, "y")
+        vals_w_g = sb.tile([P, I], U32, name="vals_w_g", tag="p_g", align_bytes=64)
         nc.vector.tensor_copy(vals_w_g[:], vals_w[:].bitcast(U32).indirect(list0[:]))
+        gout_q = quantize("gout", gout_woven, Q)
         c0 = product("c0", gout_q, (vals_w_g[:], vals_sc_g[:]), I)
 
-        r = wide("r")
-        r_sum = col("r_sum")
-        nc.vector.scalar_tensor_tensor(r[:], pr[:], 1.0, inv[:], ALU.mult, ALU.mult, accum_out=r_sum[:])
-        tden = wide("tden")
-        for h in HALVES:
-            nc.vector.scalar_tensor_tensor(tden[:, h], tp[:, h], inv_rival[:], tp_g[:, h], ALU.mult, ALU.add)
-        alpha = col("alpha")
-        nc.vector.reciprocal(alpha[:], r_sum[:])
+        r = wide("r", tag="vals_w")
+        r_sum = col("r_sum", tag="vals_sc")
+        nc.vector.scalar_tensor_tensor(r[:], p[:, :I], 1.0, inv[:], ALU.mult, ALU.mult, accum_out=r_sum[:])
         rc = wide("rc")
         rc_sum = col("rc_sum")
         nc.vector.scalar_tensor_tensor(rc[:], c0[:], -1.0, r[:], ALU.mult, ALU.mult, accum_out=rc_sum[:])
+        alpha = col("alpha")
+        nc.vector.reciprocal(alpha[:], r_sum[:])
+        tden = wide("tden")
+        for h in HALVES:
+            nc.vector.scalar_tensor_tensor(tden[:, h], tp_g[:, h], rival_c[:], tp[:, h], ALU.mult, ALU.add)
         sq = wide("sq")
         nc.scalar.activation(sq[:], r[:], ACT.Square, bias=-0.5)
         neg_mu = col("neg_mu")

from contextlib import ExitStack

import concourse.mybir as mybir

D, T, I, Q, U = 512, 2048, 512, 128, 1024
FLOPS = 4 * 2 * D * Q * I

F32 = mybir.dt.float32
BF16 = mybir.dt.bfloat16
I32 = mybir.dt.int32
U32 = mybir.dt.uint32
U16 = mybir.dt.uint16
U8 = mybir.dt.uint8
FP8X4 = mybir.dt.float8_e4m3fn_x4
ALU = mybir.AluOpType
ACT = mybir.ActivationFunctionType

P = 128
PACK = 4
SPARE = 16
SCALAR_SLOTS = 320
HALF = I // 2
HALVES = (slice(0, HALF), slice(HALF, I))
OUT_CUTS = (0, 256, 768, 1280, 1792, 2048)


def tile_attend_hvtilted_overlinked_s_kernel(tc, query, query2, keys_words, keys_scales, notes, lam, rival, gout,
                                              vals_words, vals_scales, dquery, base, offs2, offs4, offs, out):
    nc = tc.nc
    with ExitStack() as ctx:
        sb = ctx.enter_context(tc.tile_pool(name="sb", bufs=1))
        ps = ctx.enter_context(tc.psum_pool(name="ps", bufs=1))

        def wide(name, cols=I, tag=None):
            return sb.tile([P, cols], F32, name=name, tag=tag or name, align_bytes=64)

        def col(name, tag=None):
            return sb.tile([P, 1], F32, name=name, tag=tag or name, align_bytes=64)

        def load_list(name, src):
            t = sb.tile([P, I // 16], U16, name=name)
            nc.sync.dma_start(t[:], src)
            return t

        def load_rows(name, src, tag=None):
            t = sb.tile([P, PACK, Q], F32, name=name, tag=tag or name, align_bytes=64)
            nc.sync.dma_start(t[:], src.rearrange("(p j) w -> p j w", j=PACK))
            return t

        def load_words(name, src, tag=None):
            t = sb.tile([P, T], I32, name=name, tag=tag or name, align_bytes=64)
            nc.sync.dma_start(t[:], src[0].rearrange("p n t -> p (n t)").bitcast(I32))
            return t

        def zeroed_plane(name):
            t = sb.tile([P, T], U8, name=name, align_bytes=64)
            nc.vector.memset(t[:].bitcast(I32), 0)
            return t

        def load_scales(t, src, queue):
            for quad in range(4):
                queue.dma_start(t[32 * quad:32 * quad + 4, :].bitcast(I32),
                                    src[0, 4 * quad:4 * quad + 4, :].bitcast(I32))

        def weave_views(dst, src):
            return (dst.rearrange("p (c i) t -> p c t i", i=4), src.rearrange("p t (c i) -> p c t i", i=4))

        def quantize(name, woven, cols):
            codes = sb.tile([P, cols], U32, name=name + "_codes", align_bytes=64)
            scales = sb.tile([P, cols], U8, name=name + "_scales", align_bytes=64)
            nc.vector.quantize_mx(out=codes[:].bitcast(FP8X4), scales=scales[:],
                                  in_=woven[:].rearrange("p w j -> p (w j)"))
            return codes[:], scales[:]

        def weave_rows(name, raw, on_scalar, tag=None):
            woven = sb.tile([P, Q, PACK], BF16, name=name + "_woven", tag=tag or name + "_woven", align_bytes=64)
            dst, src = weave_views(woven[:], raw[:])
            if on_scalar:
                nc.scalar.activation(dst, src, ACT.Copy)
            else:
                nc.vector.tensor_copy(dst, src)
            return woven

        def product(name, rows, cols, width):
            acc = ps.tile([P, width], F32, name=name)
            nc.tensor.matmul_mx(out=acc[:], lhsT=rows[0].bitcast(FP8X4), lhsT_scale=rows[1],
                                rhs=cols[0].bitcast(FP8X4), rhs_scale=cols[1], start=True, stop=True)
            return acc

        def entries(lst, slots):
            return lst[:, slots.start // 16:slots.stop // 16]

        def load_plane(t):
            plane = wide("plane%d" % t, U)
            nc.sync.dma_start(plane[:], notes.rearrange("(p j) u -> p j u", j=PACK)[:, t, :])
            return plane

        warm_in = col("warm_in")
        nc.gpsimd.memset(warm_in[:], 0.0)
        warm_out = col("warm_out")
        nc.scalar.activation(warm_out[:], warm_in[:], ACT.Exp)
        keys_sc = zeroed_plane("keys_sc")
        vals_sc = zeroed_plane("vals_sc")
        load_scales(vals_sc, vals_scales, nc.gpsimd)
        list2 = load_list("list2", offs2)
        planes = [load_plane(0), load_plane(1)]
        load_scales(keys_sc, keys_scales, nc.sync)
        list0 = load_list("list0", offs)
        planes.extend([load_plane(2), load_plane(3)])
        query2_raw = load_rows("query2_raw", query2)
        query_raw = load_rows("query_raw", query)
        keys_w = load_words("keys_w", keys_words)
        dquery_raw = load_rows("dquery_raw", dquery)
        lam_c = col("lam_c")
        nc.sync.dma_start(lam_c[:], lam)
        list4 = load_list("list4", offs4)
        rival_c = col("rival_c")
        nc.sync.dma_start(rival_c[:], rival)
        gout_raw = load_rows("gout_raw", gout)
        vals_w = load_words("vals_w", vals_words)

        p = wide("p", I + SPARE)
        tp = wide("tp", I + SPARE)
        back_s = wide("back_s")
        back_v = wide("back_v")
        gf = wide("gf", T)
        nc.vector.memset(p[:, I:], 0.0)
        nc.vector.memset(tp[:, I:], 0.0)
        nc.vector.memset(back_s[:], 0.0)
        nc.vector.memset(back_v[:], 0.0)
        nc.vector.memset(gf[:], 0.0)

        keys_sc_g = sb.tile([P, I], U8, name="keys_sc_g", align_bytes=64)
        nc.vector.tensor_copy(keys_sc_g[:], keys_sc[:].indirect(list0[:]))

        notes_g = sb.tile([P, PACK, I], BF16, name="notes_g", align_bytes=64)
        for t in range(PACK - 1):
            nc.scalar.activation(notes_g[:, t, :], planes[t][:].indirect(list2[:]), ACT.Copy)
        for h in HALVES:
            nc.scalar.activation(notes_g[:, PACK - 1, h], planes[PACK - 1][:].indirect(entries(list2, h)), ACT.Copy)
        query2_woven = weave_rows("query2", query2_raw, True)
        query_woven = weave_rows("query", query_raw, True)
        notes_woven = []
        for k, h in enumerate(HALVES):
            woven = sb.tile([P, HALF, PACK], BF16, name="notes_woven%d" % k, align_bytes=64)
            nc.vector.tensor_copy(*weave_views(woven[:], notes_g[:, :, h]))
            notes_woven.append(woven)
        query2_q = quantize("query2", query2_woven, Q)
        b = [product("b%d" % k, query2_q, quantize("notes%d" % k, notes_woven[k], HALF), HALF) for k in range(2)]
        query_q = quantize("query", query_woven, Q)

        tanh_b = wide("tanh_b")
        gate = wide("gate")
        for k, h in enumerate(HALVES):
            nc.scalar.activation(tanh_b[:, h], b[k][:], ACT.Tanh, scale=0.5)
        for h in HALVES:
            nc.scalar.activation(gate[:, h], tanh_b[:, h], ACT.Identity, scale=-0.5 / HALF, bias=-0.5 / HALF)

        keys_q = []
        a = []
        for k, h in enumerate(HALVES):
            words = sb.tile([P, HALF], U32, name="keys_w_g%d" % k, tag="notes_woven%d" % k, align_bytes=64)
            nc.vector.tensor_copy(words[:], keys_w[:].bitcast(U32).indirect(entries(list0, h)))
            keys_q.append((words[:], keys_sc_g[:, h]))
            a.append(product("a%d" % k, query_q, keys_q[k], HALF))
        dquery_woven = weave_rows("dquery", dquery_raw, True, "tanh_b")

        base_sb = wide("base_sb", T, "keys_w")
        nc.sync.dma_start(base_sb[:], base)

        y = wide("y")
        shift = col("shift")
        nc.vector.scalar_tensor_tensor(y[:, HALVES[0]], a[0][:], lam_c[:], gate[:, HALVES[0]], ALU.subtract, ALU.mult,
                                       accum_out=shift[:])
        nc.vector.scalar_tensor_tensor(y[:, HALVES[1]], a[1][:], lam_c[:], gate[:, HALVES[1]], ALU.subtract, ALU.mult)
        for h in HALVES:
            nc.scalar.activation(p[:, h], y[:, h], ACT.Exp, scale=-float(HALF), bias=shift[:])
        p_g = wide("p_g")
        for h in HALVES:
            nc.scalar.activation(p_g[:, h], p[:].indirect(entries(list4, h)), ACT.Copy)
        warm_root = col("warm_root")
        nc.scalar.activation(warm_root[:], p_g[:, I - 1:I], ACT.Abs_reciprocal_sqrt)
        dquery_q = quantize("dquery", dquery_woven, Q)
        ta = [product("ta%d" % k, dquery_q, keys_q[k], HALF) for k in range(2)]
        vals_sc_g = sb.tile([P, I], U8, name="vals_sc_g", tag="lam_c", align_bytes=64)
        nc.vector.tensor_copy(vals_sc_g[:], vals_sc[:].indirect(list0[:]))
        den = wide("den")
        root = wide("root")
        inv = wide("inv")
        ts = wide("ts")
        for k, h in enumerate(HALVES):
            nc.vector.tensor_tensor(ts[:, h], ta[k][:], gate[:, h], ALU.mult)
        nc.vector.scalar_tensor_tensor(den[:], p_g[:], rival_c[:], p[:, :I], ALU.mult, ALU.add)
        for h in HALVES:
            nc.scalar.activation(root[:, h], den[:, h], ACT.Abs_reciprocal_sqrt)
        for h in HALVES:
            nc.scalar.activation(inv[:, h], root[:, h], ACT.Square)
        nc.vector.tensor_tensor(tp[:, :I], ts[:], p[:, :I], ALU.mult)
        tp_g = wide("tp_g", tag="root")
        for h in HALVES:
            nc.scalar.activation(tp_g[:, h], tp[:].indirect(entries(list4, h)), ACT.Copy)

        gout_woven = weave_rows("gout", gout_raw, False, "y")
        vals_w_g = sb.tile([P, I], U32, name="vals_w_g", tag="p_g", align_bytes=64)
        nc.vector.tensor_copy(vals_w_g[:], vals_w[:].bitcast(U32).indirect(list0[:]))
        gout_q = quantize("gout", gout_woven, Q)
        c0 = product("c0", gout_q, (vals_w_g[:], vals_sc_g[:]), I)

        r = wide("r", tag="vals_w")
        r_sum = col("r_sum", tag="vals_sc")
        nc.vector.scalar_tensor_tensor(r[:], p[:, :I], 1.0, inv[:], ALU.mult, ALU.mult, accum_out=r_sum[:])
        rc = wide("rc")
        rc_sum = col("rc_sum")
        nc.vector.scalar_tensor_tensor(rc[:], c0[:], -1.0, r[:], ALU.mult, ALU.mult, accum_out=rc_sum[:])
        alpha = col("alpha")
        nc.vector.reciprocal(alpha[:], r_sum[:])
        tden = wide("tden")
        for h in HALVES:
            nc.vector.scalar_tensor_tensor(tden[:, h], tp_g[:, h], rival_c[:], tp[:, h], ALU.mult, ALU.add)
        sq = wide("sq")
        nc.scalar.activation(sq[:], r[:], ACT.Square, bias=-0.5)
        neg_mu = col("neg_mu")
        nc.scalar.activation(neg_mu[:], rc_sum[:], ACT.Identity, scale=alpha[:])
        c1 = wide("c1")
        nc.scalar.activation(c1[:], c0[:], ACT.Identity, bias=neg_mu[:])
        m_scale = col("m_scale")
        nc.scalar.activation(m_scale[:], alpha[:], ACT.Identity, scale=-0.5)
        m_bias = col("m_bias")
        nc.scalar.activation(m_bias[:], alpha[:], ACT.Identity, scale=0.125)
        out_scale = col("out_scale")
        nc.scalar.activation(out_scale[:], alpha[:], ACT.Identity, scale=-2.0 * 512.0 * HALF * HALF)
        half_m = wide("half_m")
        nc.scalar.activation(half_m[:], sq[:], ACT.Identity, scale=m_scale[:], bias=m_bias[:])
        e = wide("e")
        dd = wide("dd")
        tr = wide("tr")
        trc = wide("trc")
        tr_part = [col("tr_part0"), col("tr_part1")]
        trc_part = [col("trc_part0"), col("trc_part1")]
        for h in HALVES:
            nc.vector.tensor_tensor(e[:, h], tden[:, h], inv[:, h], ALU.mult)
        for h in HALVES:
            nc.vector.tensor_tensor(dd[:, h], ts[:, h], e[:, h], ALU.subtract)
        for k, h in enumerate(HALVES):
            nc.vector.scalar_tensor_tensor(tr[:, h], r[:, h], 1.0, dd[:, h], ALU.mult, ALU.mult, accum_out=tr_part[k][:])
        for k, h in enumerate(HALVES):
            nc.vector.scalar_tensor_tensor(trc[:, h], tr[:, h], 1.0, c1[:, h], ALU.mult, ALU.mult,
                                           accum_out=trc_part[k][:])
        tr_sum = col("tr_sum")
        nc.scalar.activation(tr_sum[:], tr_part[0][:], ACT.Identity, bias=tr_part[1][:])
        first = slice(0, SCALAR_SLOTS)
        rest = slice(SCALAR_SLOTS, I)
        c2 = wide("c2")
        for h in (first, rest):
            nc.scalar.activation(c2[:, h], c1[:, h], ACT.Identity, scale=tr_sum[:], bias=trc_part[0][:])
        w = wide("w")
        z = wide("z")
        th = wide("th")
        for h in (first, rest):
            nc.vector.scalar_tensor_tensor(w[:, h], r[:, h], -0.5, trc[:, h], ALU.add, ALU.mult)
        for h in (first, rest):
            nc.vector.scalar_tensor_tensor(z[:, h], c2[:, h], trc_part[1][:], half_m[:, h], ALU.add, ALU.mult)
        nc.vector.tensor_tensor(th[:, first], z[:, first], w[:, first], ALU.add)
        nc.scalar.activation(back_s[:].indirect(entries(list4, first)), th[:, first], ACT.Copy)
        out_gate = wide("out_gate")
        nc.scalar.activation(out_gate[:], gate[:], ACT.Identity, scale=out_scale[:])
        nc.vector.tensor_tensor(back_v[:].indirect(entries(list4, rest)), z[:, rest], w[:, rest], ALU.add)
        nc.vector.tensor_tensor(th[:, rest], z[:, rest], w[:, rest], ALU.add)
        d1 = wide("d1")
        for h in (first, rest):
            nc.vector.tensor_tensor(d1[:, h], th[:, h], back_v[:, h], ALU.subtract)
        d2 = wide("d2")
        nc.vector.tensor_tensor(d2[:], d1[:], back_s[:], ALU.subtract)
        nc.vector.tensor_tensor(gf[:].indirect(list0[:]), d2[:], out_gate[:], ALU.mult)

        for c in range(len(OUT_CUTS) - 1):
            cols = slice(OUT_CUTS[c], OUT_CUTS[c + 1])
            res = wide("res%d" % c, cols.stop - cols.start)
            nc.vector.tensor_tensor(res[:], gf[:, cols], base_sb[:, cols], ALU.add)
            nc.sync.dma_start(out[:, cols], res[:])
